import numpy as np
import ml_dtypes

BF16 = ml_dtypes.bfloat16


def bf(x):
    return np.asarray(x, np.float32).astype(BF16)


def f32(x):
    return np.asarray(x, np.float32)


def f64(x):
    return np.asarray(x).astype(np.float64)


def striped(idx):
    return np.tile(idx.reshape(-1, 16).T, (8, 1))


S, K, M, N, H = 1024, 128, 256, 384, 128


def sigmoid(v):
    return 1.0 / (1.0 + np.exp(-v))


def setup_inputs():
    return {"table": bf(np.random.standard_normal((S, K))), "w": bf(np.random.standard_normal((K, M)) / np.sqrt(K)), "offs": striped(np.random.permutation(np.tile(np.arange(S), 2))[:N])}


def reference(table, w, offs):
    idx = offs[:16].T.reshape(-1)
    x = f64(table)[idx].T
    y = f64(w).T @ x
    return y[:H] * sigmoid(y[H:])

@@ -1,0 +1,55 @@
+import concourse.mybir as mybir
+from concourse.masks import make_identity
+
+P = 128
+S = 1024
+N = 384
+BLOCKS = S // P
+HALF = BLOCKS // 2
+
+FLOPS = 2 * P * (2 * P) * N
+
+BF16, F32, U16 = mybir.dt.bfloat16, mybir.dt.float32, mybir.dt.uint16
+SIGMOID = mybir.ActivationFunctionType.Sigmoid
+MULT = mybir.AluOpType.mult
+
+
+def tile_gather_matmul_kernel(tc, table, w, offs, out):
+    nc = tc.nc
+    with (
+        tc.tile_pool(name="held", bufs=1) as held,
+        tc.psum_pool(name="flipped", bufs=1) as flipped,
+        tc.psum_pool(name="products", bufs=1) as products,
+    ):
+        offsets = held.tile([P, N // 16], U16, name="offsets")
+        words = held.tile([P, BLOCKS, P], BF16, name="words")
+        weights = held.tile([P, 2 * P], BF16, name="weights")
+        by_block = table.rearrange("(a p) k -> p a k", p=P)
+        nc.sync.dma_start(words[:, 0:HALF, :], by_block[:, 0:HALF, :])
+        nc.scalar.dma_start(words[:, HALF:BLOCKS, :], by_block[:, HALF:BLOCKS, :])
+        nc.sync.dma_start(offsets[:], offs)
+        nc.scalar.dma_start(weights[:], w)
+
+        identity = held.tile([P, P], BF16, name="identity")
+        make_identity(nc, identity[:])
+
+        table_t = held.tile([P, S], BF16, name="table_t")
+        low = flipped.tile([P, HALF * P], BF16, name="low")
+        high = flipped.tile([P, HALF * P], BF16, name="high")
+        for a in range(HALF):
+            nc.tensor.transpose(low[:, a * P : (a + 1) * P], words[:, a, :], identity[:])
+        nc.vector.tensor_copy(table_t[:, 0 : HALF * P], low[:])
+        for a in range(HALF):
+            nc.tensor.transpose(high[:, a * P : (a + 1) * P], words[:, HALF + a, :], identity[:])
+        nc.scalar.copy(table_t[:, HALF * P : S], high[:])
+
+        gates = products.tile([P, N], F32, name="gates")
+        values = products.tile([P, N], F32, name="values")
+        nc.tensor.matmul(gates[:], weights[:, P : 2 * P], table_t[:].indirect(offsets[:]), start=True, stop=True)
+        nc.tensor.matmul(values[:], weights[:, 0:P], table_t[:].indirect(offsets[:]), start=True, stop=True)
+
+        opened = held.tile([P, N], F32, name="opened")
+        result = held.tile([P, N], F32, name="result")
+        nc.scalar.activation(opened[:], gates[:], SIGMOID)
+        nc.vector.tensor_tensor(result[:], values[:], opened[:], MULT)
+        nc.sync.dma_start(out, result[:])

@@ -5,7 +5,10 @@ P = 128
 S = 1024
 N = 384
 BLOCKS = S // P
-HALF = BLOCKS // 2
+GROUPS = 4
+G = BLOCKS // GROUPS
+PIECES = 2
+Q = N // PIECES
 
 FLOPS = 2 * P * (2 * P) * N
 
@@ -25,31 +28,43 @@ def tile_gather_matmul_kernel(tc, table, w, offs, out):
         words = held.tile([P, BLOCKS, P], BF16, name="words")
         weights = held.tile([P, 2 * P], BF16, name="weights")
         by_block = table.rearrange("(a p) k -> p a k", p=P)
-        nc.sync.dma_start(words[:, 0:HALF, :], by_block[:, 0:HALF, :])
-        nc.scalar.dma_start(words[:, HALF:BLOCKS, :], by_block[:, HALF:BLOCKS, :])
+        load_queues = [nc.sync, nc.scalar]
+        for g in range(GROUPS):
+            blocks = slice(g * G, (g + 1) * G)
+            load_queues[g % 2].dma_start(words[:, blocks, :], by_block[:, blocks, :])
         nc.sync.dma_start(offsets[:], offs)
         nc.scalar.dma_start(weights[:], w)
+
+        warm = held.tile([P, 1], F32, name="warm")
+        nc.vector.memset(warm[:], 0.0)
+        nc.scalar.activation(warm[:], warm[:], SIGMOID)
 
         identity = held.tile([P, P], BF16, name="identity")
         make_identity(nc, identity[:])
 
         table_t = held.tile([P, S], BF16, name="table_t")
-        low = flipped.tile([P, HALF * P], BF16, name="low")
-        high = flipped.tile([P, HALF * P], BF16, name="high")
-        for a in range(HALF):
-            nc.tensor.transpose(low[:, a * P : (a + 1) * P], words[:, a, :], identity[:])
-        nc.vector.tensor_copy(table_t[:, 0 : HALF * P], low[:])
-        for a in range(HALF):
-            nc.tensor.transpose(high[:, a * P : (a + 1) * P], words[:, HALF + a, :], identity[:])
-        nc.scalar.copy(table_t[:, HALF * P : S], high[:])
+        for g in range(GROUPS):
+            bank = flipped.tile([P, G * P], BF16, name=f"bank{g}")
+            for a in range(G):
+                nc.tensor.transpose(bank[:, a * P : (a + 1) * P], words[:, g * G + a, :], identity[:])
+            columns = table_t[:, g * G * P : (g + 1) * G * P]
+            if g % 2 == 0:
+                nc.vector.tensor_copy(columns, bank[:])
+            else:
+                nc.scalar.copy(columns, bank[:])
 
-        gates = products.tile([P, N], F32, name="gates")
-        values = products.tile([P, N], F32, name="values")
-        nc.tensor.matmul(gates[:], weights[:, P : 2 * P], table_t[:].indirect(offsets[:]), start=True, stop=True)
-        nc.tensor.matmul(values[:], weights[:, 0:P], table_t[:].indirect(offsets[:]), start=True, stop=True)
+        picked = [table_t[:].indirect(offsets[:, q * (Q // 16) : (q + 1) * (Q // 16)]) for q in range(PIECES)]
+        gates = [products.tile([P, Q], F32, name=f"gates{q}") for q in range(PIECES)]
+        values = [products.tile([P, Q], F32, name=f"values{q}") for q in range(PIECES)]
+        for q in range(PIECES):
+            nc.tensor.matmul(gates[q][:], weights[:, P : 2 * P], picked[q], start=True, stop=True)
+        for q in range(PIECES):
+            nc.tensor.matmul(values[q][:], weights[:, 0:P], picked[q], start=True, stop=True)
 
-        opened = held.tile([P, N], F32, name="opened")
-        result = held.tile([P, N], F32, name="result")
-        nc.scalar.activation(opened[:], gates[:], SIGMOID)
-        nc.vector.tensor_tensor(result[:], values[:], opened[:], MULT)
-        nc.sync.dma_start(out, result[:])
+        store_queues = [nc.sync, nc.scalar]
+        for q in range(PIECES):
+            opened = held.tile([P, Q], F32, name=f"opened{q}")
+            result = held.tile([P, Q], F32, name=f"result{q}")
+            nc.scalar.activation(opened[:], gates[q][:], SIGMOID)
+            nc.vector.tensor_tensor(result[:], values[q][:], opened[:], MULT)
+            store_queues[q].dma_start(out[:, q * Q : (q + 1) * Q], result[:])

@@ -9,6 +9,8 @@ GROUPS = 4
 G = BLOCKS // GROUPS
 PIECES = 2
 Q = N // PIECES
+BANK = 512
+IDLE = 3
 
 FLOPS = 2 * P * (2 * P) * N
 
@@ -22,7 +24,6 @@ def tile_gather_matmul_kernel(tc, table, w, offs, out):
     with (
         tc.tile_pool(name="held", bufs=1) as held,
         tc.psum_pool(name="flipped", bufs=1) as flipped,
-        tc.psum_pool(name="products", bufs=1) as products,
     ):
         offsets = held.tile([P, N // 16], U16, name="offsets")
         words = held.tile([P, BLOCKS, P], BF16, name="words")
@@ -39,6 +40,13 @@ def tile_gather_matmul_kernel(tc, table, w, offs, out):
         nc.vector.memset(warm[:], 0.0)
         nc.scalar.activation(warm[:], warm[:], SIGMOID)
 
+        zeros = held.tile([P, BANK], BF16, name="zeros")
+        nc.vector.memset(zeros[:], 0.0)
+        with tc.psum_pool(name="idle", bufs=1) as idle:
+            unused = idle.tile([P, BANK], F32, name="unused")
+            for i in range(IDLE):
+                nc.tensor.matmul(unused[:], zeros[:, 0:P], zeros[:], start=True, stop=True)
+
         identity = held.tile([P, P], BF16, name="identity")
         make_identity(nc, identity[:])
 
@@ -53,18 +61,19 @@ def tile_gather_matmul_kernel(tc, table, w, offs, out):
             else:
                 nc.scalar.copy(columns, bank[:])
 
-        picked = [table_t[:].indirect(offsets[:, q * (Q // 16) : (q + 1) * (Q // 16)]) for q in range(PIECES)]
-        gates = [products.tile([P, Q], F32, name=f"gates{q}") for q in range(PIECES)]
-        values = [products.tile([P, Q], F32, name=f"values{q}") for q in range(PIECES)]
-        for q in range(PIECES):
-            nc.tensor.matmul(gates[q][:], weights[:, P : 2 * P], picked[q], start=True, stop=True)
-        for q in range(PIECES):
-            nc.tensor.matmul(values[q][:], weights[:, 0:P], picked[q], start=True, stop=True)
+        with tc.psum_pool(name="products", bufs=1) as products:
+            picked = [table_t[:].indirect(offsets[:, q * (Q // 16) : (q + 1) * (Q // 16)]) for q in range(PIECES)]
+            gates = [products.tile([P, Q], F32, name=f"gates{q}") for q in range(PIECES)]
+            values = [products.tile([P, Q], F32, name=f"values{q}") for q in range(PIECES)]
+            for q in range(PIECES):
+                nc.tensor.matmul(gates[q][:], weights[:, P : 2 * P], picked[q], start=True, stop=True)
+            for q in range(PIECES):
+                nc.tensor.matmul(values[q][:], weights[:, 0:P], picked[q], start=True, stop=True)
 
-        store_queues = [nc.sync, nc.scalar]
-        for q in range(PIECES):
-            opened = held.tile([P, Q], F32, name=f"opened{q}")
-            result = held.tile([P, Q], F32, name=f"result{q}")
-            nc.scalar.activation(opened[:], gates[q][:], SIGMOID)
-            nc.vector.tensor_tensor(result[:], values[q][:], opened[:], MULT)
-            store_queues[q].dma_start(out[:, q * Q : (q + 1) * Q], result[:])
+            store_queues = [nc.sync, nc.scalar]
+            for q in range(PIECES):
+                opened = held.tile([P, Q], F32, name=f"opened{q}")
+                result = held.tile([P, Q], F32, name=f"result{q}")
+                nc.scalar.activation(opened[:], gates[q][:], SIGMOID)
+                nc.vector.tensor_tensor(result[:], values[q][:], opened[:], MULT)
+                store_queues[q].dma_start(out[:, q * Q : (q + 1) * Q], result[:])

@@ -10,7 +10,7 @@ G = BLOCKS // GROUPS
 PIECES = 2
 Q = N // PIECES
 BANK = 512
-IDLE = 3
+IDLE = 2
 
 FLOPS = 2 * P * (2 * P) * N
 
@@ -36,16 +36,18 @@ def tile_gather_matmul_kernel(tc, table, w, offs, out):
         nc.sync.dma_start(offsets[:], offs)
         nc.scalar.dma_start(weights[:], w)
 
+        zeros = held.tile([P, P], BF16, name="zeros")
+        nc.vector.memset(zeros[:], 0.0)
+        with tc.psum_pool(name="idle", bufs=1) as idle:
+            unused = idle.tile([P, BANK // P, P], F32, name="unused")
+            for i in range(IDLE):
+                nc.tensor.matmul(
+                    unused[:], zeros[:], zeros[:].unsqueeze(1).to_broadcast([P, BANK // P, P]), start=True, stop=True
+                )
+
         warm = held.tile([P, 1], F32, name="warm")
         nc.vector.memset(warm[:], 0.0)
         nc.scalar.activation(warm[:], warm[:], SIGMOID)
-
-        zeros = held.tile([P, BANK], BF16, name="zeros")
-        nc.vector.memset(zeros[:], 0.0)
-        with tc.psum_pool(name="idle", bufs=1) as idle:
-            unused = idle.tile([P, BANK], F32, name="unused")
-            for i in range(IDLE):
-                nc.tensor.matmul(unused[:], zeros[:, 0:P], zeros[:], start=True, stop=True)
 
         identity = held.tile([P, P], BF16, name="identity")
         make_identity(nc, identity[:])

@@ -7,7 +7,7 @@ N = 384
 BLOCKS = S // P
 GROUPS = 4
 G = BLOCKS // GROUPS
-PIECES = 2
+PIECES = 3
 Q = N // PIECES
 BANK = 512
 IDLE = 2
@@ -21,10 +21,7 @@ MULT = mybir.AluOpType.mult
 
 def tile_gather_matmul_kernel(tc, table, w, offs, out):
     nc = tc.nc
-    with (
-        tc.tile_pool(name="held", bufs=1) as held,
-        tc.psum_pool(name="flipped", bufs=1) as flipped,
-    ):
+    with tc.tile_pool(name="held", bufs=1) as held:
         offsets = held.tile([P, N // 16], U16, name="offsets")
         words = held.tile([P, BLOCKS, P], BF16, name="words")
         weights = held.tile([P, 2 * P], BF16, name="weights")
@@ -53,15 +50,16 @@ def tile_gather_matmul_kernel(tc, table, w, offs, out):
         make_identity(nc, identity[:])
 
         table_t = held.tile([P, S], BF16, name="table_t")
-        for g in range(GROUPS):
-            bank = flipped.tile([P, G * P], BF16, name=f"bank{g}")
-            for a in range(G):
-                nc.tensor.transpose(bank[:, a * P : (a + 1) * P], words[:, g * G + a, :], identity[:])
-            columns = table_t[:, g * G * P : (g + 1) * G * P]
-            if g % 2 == 0:
-                nc.vector.tensor_copy(columns, bank[:])
-            else:
-                nc.scalar.copy(columns, bank[:])
+        with tc.psum_pool(name="flipped", bufs=1) as flipped:
+            for g in range(GROUPS):
+                bank = flipped.tile([P, G * P], BF16, name=f"bank{g}")
+                for a in range(G):
+                    nc.tensor.transpose(bank[:, a * P : (a + 1) * P], words[:, g * G + a, :], identity[:])
+                columns = table_t[:, g * G * P : (g + 1) * G * P]
+                if g % 2 == 0:
+                    nc.vector.tensor_copy(columns, bank[:])
+                else:
+                    nc.scalar.copy(columns, bank[:])
 
         with tc.psum_pool(name="products", bufs=1) as products:
             picked = [table_t[:].indirect(offsets[:, q * (Q // 16) : (q + 1) * (Q // 16)]) for q in range(PIECES)]
@@ -72,10 +70,12 @@ def tile_gather_matmul_kernel(tc, table, w, offs, out):
             for q in range(PIECES):
                 nc.tensor.matmul(values[q][:], weights[:, 0:P], picked[q], start=True, stop=True)
 
-            store_queues = [nc.sync, nc.scalar]
+            early = held.tile([P, (PIECES - 1) * Q], F32, name="early")
+            late = held.tile([P, Q], F32, name="late")
             for q in range(PIECES):
                 opened = held.tile([P, Q], F32, name=f"opened{q}")
-                result = held.tile([P, Q], F32, name=f"result{q}")
+                result = late[:] if q == PIECES - 1 else early[:, q * Q : (q + 1) * Q]
                 nc.scalar.activation(opened[:], gates[q][:], SIGMOID)
-                nc.vector.tensor_tensor(result[:], values[q][:], opened[:], MULT)
-                store_queues[q].dma_start(out[:, q * Q : (q + 1) * Q], result[:])
+                nc.vector.tensor_tensor(result, values[q][:], opened[:], MULT)
+            nc.sync.dma_start(out[:, 0 : (PIECES - 1) * Q], early[:])
+            nc.scalar.dma_start(out[:, (PIECES - 1) * Q : N], late[:])

import concourse.mybir as mybir
from concourse.masks import make_identity

P = 128
S = 1024
N = 384
BLOCKS = S // P
GROUPS = 4
G = BLOCKS // GROUPS
PIECES = 3
Q = N // PIECES
BANK = 512
IDLE = 2

FLOPS = 2 * P * (2 * P) * N

BF16, F32, U16 = mybir.dt.bfloat16, mybir.dt.float32, mybir.dt.uint16
SIGMOID = mybir.ActivationFunctionType.Sigmoid
MULT = mybir.AluOpType.mult


def tile_gather_matmul_kernel(tc, table, w, offs, out):
    nc = tc.nc
    with tc.tile_pool(name="held", bufs=1) as held:
        offsets = held.tile([P, N // 16], U16, name="offsets")
        words = held.tile([P, BLOCKS, P], BF16, name="words")
        weights = held.tile([P, 2 * P], BF16, name="weights")
        by_block = table.rearrange("(a p) k -> p a k", p=P)
        load_queues = [nc.sync, nc.scalar]
        for g in range(GROUPS):
            blocks = slice(g * G, (g + 1) * G)
            load_queues[g % 2].dma_start(words[:, blocks, :], by_block[:, blocks, :])
        nc.sync.dma_start(offsets[:], offs)
        nc.scalar.dma_start(weights[:], w)

        zeros = held.tile([P, P], BF16, name="zeros")
        nc.vector.memset(zeros[:], 0.0)
        with tc.psum_pool(name="idle", bufs=1) as idle:
            unused = idle.tile([P, BANK // P, P], F32, name="unused")
            for i in range(IDLE):
                nc.tensor.matmul(
                    unused[:], zeros[:], zeros[:].unsqueeze(1).to_broadcast([P, BANK // P, P]), start=True, stop=True
                )

        warm = held.tile([P, 1], F32, name="warm")
        nc.vector.memset(warm[:], 0.0)
        nc.scalar.activation(warm[:], warm[:], SIGMOID)

        identity = held.tile([P, P], BF16, name="identity")
        make_identity(nc, identity[:])

        table_t = held.tile([P, S], BF16, name="table_t")
        with tc.psum_pool(name="flipped", bufs=1) as flipped:
            for g in range(GROUPS):
                bank = flipped.tile([P, G * P], BF16, name=f"bank{g}")
                for a in range(G):
                    nc.tensor.transpose(bank[:, a * P : (a + 1) * P], words[:, g * G + a, :], identity[:])
                columns = table_t[:, g * G * P : (g + 1) * G * P]
                if g % 2 == 0:
                    nc.vector.tensor_copy(columns, bank[:])
                else:
                    nc.scalar.copy(columns, bank[:])

        with tc.psum_pool(name="products", bufs=1) as products:
            picked = [table_t[:].indirect(offsets[:, q * (Q // 16) : (q + 1) * (Q // 16)]) for q in range(PIECES)]
            gates = [products.tile([P, Q], F32, name=f"gates{q}") for q in range(PIECES)]
            values = [products.tile([P, Q], F32, name=f"values{q}") for q in range(PIECES)]
            for q in range(PIECES):
                nc.tensor.matmul(gates[q][:], weights[:, P : 2 * P], picked[q], start=True, stop=True)
            for q in range(PIECES):
                nc.tensor.matmul(values[q][:], weights[:, 0:P], picked[q], start=True, stop=True)

            early = held.tile([P, (PIECES - 1) * Q], F32, name="early")
            late = held.tile([P, Q], F32, name="late")
            for q in range(PIECES):
                opened = held.tile([P, Q], F32, name=f"opened{q}")
                result = late[:] if q == PIECES - 1 else early[:, q * Q : (q + 1) * Q]
                nc.scalar.activation(opened[:], gates[q][:], SIGMOID)
                nc.vector.tensor_tensor(result, values[q][:], opened[:], MULT)
            nc.sync.dma_start(out[:, 0 : (PIECES - 1) * Q], early[:])
            nc.scalar.dma_start(out[:, (PIECES - 1) * Q : N], late[:])
